import numpy as np, ml_dtypes
CORES = [23,119,17,113]
N = 4
BF = ml_dtypes.bfloat16
def f(rng, *shape):
    return (rng.standard_normal(shape, dtype=np.float32) * np.exp2(rng.integers(-2, 3, shape[:-1] + (1,)))).astype(BF)
def wide(rng, *shape):
    v = f(rng, *shape).astype(np.float32); k = shape[:-2] + (1, shape[-1])
    return (v * np.exp2(rng.integers(-6, 7, k)) * (rng.random(k) > 0.0625)).astype(BF)
def gentries(a):
    return np.ascontiguousarray(a.reshape(8, 16, -1).transpose(0, 2, 1)).reshape(8, -1)
def gtable(e):
    e = np.asarray(e); return np.ascontiguousarray(e.reshape(8, -1, 16).transpose(0, 2, 1)).reshape(128, -1).astype(np.int32)
E, M, CAPP, R = 4096, 4928, 128, 2
GX, GY, GZ = 16, 16, 16
def mesh(rng):
    return np.stack([np.stack([rng.permutation(M)[:E] for c in range(8)]) for r in range(N)])
def counts(rng, lo):
    n = np.triu(rng.integers(lo, CAPP + 1, (N, N)), 1); r = int(rng.integers(0, N - 1)); n[r, int(rng.integers(r + 1, N))] = CAPP; return n
def several(rng, k):
    return [sorted(rng.choice(N, int(j), replace=False).tolist()) for j in rng.integers(3, N + 1, k)]
def shares(rng, num, sets, pool):
    h = np.tile(M + np.arange(CAPP), (N, 8, 1)); left = np.array(num); at = [0] * N; same = []
    free = {(r, q): rng.permutation(CAPP).tolist() for r in range(N) for q in range(r + 1, N)}
    def join(S):
        n = [int(pool[r][at[r]]) for r in S]
        for i, r in enumerate(S):
            at[r] += 1
            for j in range(i + 1, len(S)):
                q = S[j]; k = free[r, q].pop(); h[r, q, k] = n[i]; h[q, r, k] = n[j]; left[r, q] -= 1
            if i: same.append((S[0], n[0], r, n[i]))
    for S in sets:
        if all(left[S[i], S[j]] > 0 for i in range(len(S)) for j in range(i + 1, len(S))): join(S)
    for r in range(N):
        for q in range(r + 1, N):
            for i in range(int(left[r, q])): join([r, q])
    return h, same
def make(rng, c, hs, u, st):
    h, same = hs; w = ((0.5 + rng.random((N, 1, M))) * 0.125).astype(BF); u = np.array(u)
    for r, n, q, m in same:
        u[q, :, m] = u[r, :, n]; w[q, 0, m] = w[r, 0, n]
    return {"u": u, "w": w, "ke": rng.standard_normal((N, 8, 8)).astype(BF), "st": st.astype(BF), "conn": np.stack([gtable(a) for a in c]), "share": np.stack([gtable(a) for a in h])}
def setup_inputs(rng):
    c = mesh(rng); hs = shares(rng, counts(rng, CAPP // 2), several(rng, CAPP // 2), [rng.permutation(M) for r in range(N)])
    return make(rng, c, hs, f(rng, N, 16, M), 0.5 + rng.random((N, 1, E)))
def setup_inputs_grid(rng):
    e = np.arange(E); x, y, z = e % GX, e // GX % GY, e // (GX * GY)
    c = np.stack([((z + (k >> 2)) * (GY + 1) + y + (k >> 1 & 1)) * (GX + 1) + x + (k & 1) for k in range(8)])
    n = np.arange((GX + 1) * (GY + 1) * (GZ + 1)); x, y, z = n % (GX + 1), n // (GX + 1) % (GY + 1), n // ((GX + 1) * (GY + 1))
    n = n[(x == 0) | (x == GX) | (y == 0) | (y == GY) | (z == 0) | (z == GZ)]
    b = rng.integers(0, M - (GX + 1) * (GY + 1) * (GZ + 1) + 1, N)
    hs = shares(rng, counts(rng, 1), several(rng, CAPP // 4), [b[r] + rng.permutation(n) for r in range(N)])
    return make(rng, np.stack([c + b[r] for r in range(N)]), hs, f(rng, N, 16, M), 0.5 + rng.random((N, 1, E)))
def setup_inputs_all(rng):
    hs = shares(rng, np.triu(np.full((N, N), CAPP), 1), [list(range(N))] * CAPP, [rng.permutation(M) for r in range(N)])
    return make(rng, mesh(rng), hs, f(rng, N, 16, M), 0.5 + rng.random((N, 1, E)))
def setup_inputs_few(rng):
    n = np.zeros((N, N), np.int64)
    for q in range(1, N): n[q - 1, q] = rng.integers(0, 4)
    r = int(rng.integers(0, N - 1)); q = int(rng.integers(r + 1, N)); n[r, q] = CAPP
    inner = np.arange(1, M - 1); pool = [np.concatenate([[0, M - 1], rng.permutation(inner)]) for k in range(N)]
    c = np.zeros((N, 8, E), np.int64)
    for k in range(N):
        for a in range(8): c[k, a] = np.concatenate([[M - 1 if a % 2 else 0], rng.permutation(inner)[:E - 2], [0 if a % 2 else M - 1]])
    k = (r, q)[int(rng.integers(0, 2))]; c[k] = c[k, :1]
    return make(rng, c, shares(rng, n, [], pool), f(rng, N, 16, M), 0.5 + rng.random((N, 1, E)))
def setup_inputs_spread(rng):
    c = mesh(rng); hs = shares(rng, counts(rng, CAPP // 4), several(rng, CAPP), [rng.permutation(M) for r in range(N)])
    return make(rng, c, hs, wide(rng, N, 16, M), np.exp2(rng.integers(-2, 3, (N, 1, E))) * (rng.random((N, 1, E)) > 0.0625))
def check_inputs(d):
    bad = []; c = np.stack([gentries(a) for a in d["conn"]]).astype(np.int64); h = np.stack([gentries(a) for a in d["share"]]).astype(np.int64)
    if not all(np.isfinite(d[k].astype(np.float32)).all() for k in ("u", "w", "ke", "st")): bad.append("finite")
    if c.min() < 0 or c.max() >= M: bad.append("conn_in_range")
    t = np.sort(c, -1)
    if (t[..., 1:] == t[..., :-1]).any(): bad.append("a_node_is_corner_c_of_one_element_at_most")
    used = (h >= 0) & (h < M)
    if not (used | (h == M + np.arange(CAPP))).all(): return bad + ["share_in_range"]
    t = np.sort(h, -1)
    if (t[..., 1:] == t[..., :-1]).any(): return bad + ["a_node_stands_once_in_a_pairs_slots"]
    if used[:, N:].any() or any(used[r, r].any() for r in range(N)): return bad + ["own_and_unused_groups_empty"]
    if not (used[:, :N] == used[:, :N].transpose(1, 0, 2)).all(): return bad + ["slots_in_use_on_both_sides"]
    cp = np.full((N, M, N), -1, np.int64); alike = True
    for r in range(N):
        cp[r, :, r] = np.arange(M)
        for q in range(N):
            if q != r:
                k = used[r, q]; a, b = h[r, q][k], h[q, r][k]; cp[r, a, q] = b
                alike = alike and bool((d["u"][r][:, a] == d["u"][q][:, b]).all() and (d["w"][r][:, a] == d["w"][q][:, b]).all())
    if not alike: bad.append("copies_alike")
    if not all((cp[r, h[r, q][used[r, q]]] == cp[q, h[q, r][used[q, r]]]).all() for r in range(N) for q in range(N) if q != r): bad.append("all_copies_listed")
    return bad
def reference(u, w, ke, st, conn, share):
    c = [gentries(a) for a in conn]; h = [gentries(a) for a in share]
    x = u.astype(np.float64); wt = w.astype(np.float64); km = ke.astype(np.float64); sf = st.astype(np.float64)
    for t in range(R):
        p = np.zeros((N, 16, M + CAPP), np.float64)
        for r in range(N):
            v = np.einsum('ab,lbe->lae', km[r], x[r][:, c[r]]) * sf[r]
            for a in range(8): p[r][:, c[r][a]] += v[:, a]
        z = np.array(p)
        for r in range(N):
            for q in range(N):
                if q != r: z[r][:, h[r][q]] += p[q][:, h[q][r]]
        x = x - wt * z[:, :, :M]
    return {"y": x.astype(np.float32)}

import numpy as np
from concourse.bass import DstId, RemoteDMATransfer, IndirectOffsetOnAxis
from concourse.mybir import dt, AluOpType, AxisListType, ActivationFunctionType

A = AluOpType
F = ActivationFunctionType
E, M, CAPP = 4096, 4928, 128
MW = M + CAPP
RUN = MW // 16
NK = M // 16
ES = 2304
CB = 640
YW = CB + CAPP
PER = 4

_F = "float32 "
_B = "bfloat16 "
_I = "int32 "
_U = "uint16 "
_SB = {
    256: _I + "connI piI " + _U + "connU piU " + _F + "piN piT",
    MW: _B + "uwin wrep " + _F + "Wv Ws win ADD",
    E: _B + "strep X1 " + _F + "X2", ES: _F + "dat", E + 8: _F + "V", 8 * CB: _F + "G",
    NK: _F + "invV invS invT", 320: _U + "invU invP",
    128: _I + "idm idt asI asJ " + _F + "PosR NegR IdF KlF Rw " + _B + "IdB asB Yb KlB",
    2: _I + "pI g16 zI", 8: _F + "mk " + _B + "keB " + _I + "shI " + _U + "shU",
    24: _F + "shM SRf sqN sqT dmp0 dmp c1 c2 c3 c4 " + _I + "SRi sqI " + _U + "SRu piS clU cpU",
    384: _F + "O1 O2 Om uslot wslot S1 D1 x2s x3s", 48: _F + "send1 send2", 64: _F + "recv1 recv2",
    CB: _B + "wc wT " + _F + "x2c xT yt yu", YW: _F + "Y",
}
SCRATCH = {}
for _n in _SB:
    _t = ""
    for _w in _SB[_n].split():
        if _w + " " in (_F, _B, _I, _U):
            _t = _w
        else:
            SCRATCH[_w] = ("sbuf", [128, _n], _t)
for _k in range(8):
    SCRATCH["pb%d" % _k] = ("psum", [128, 512], "float32")

SEMAPHORES = ["cv", "cs", "ct", "cg", "dconn", "dshare", "dke", "du", "dstr", "dwr", "dxv", "dxs", "dwc", "dx2", "dy",
              "arr1", "arr2", "loc1", "loc2"]


def rank_program(g, core, T, topo):
    r = T.rank_of(core)
    if r is None:
        return
    partners = [q for q in range(len(T.cores)) if q != r]
    queue = {"v": g.vector, "s": g.scalar, "t": g.tensor, "g": g, "y": g.sync}
    count = {}
    seen = {}
    past = {}

    def wait(q, toks):
        best = {}
        for name, val in toks:
            best[name] = max(best.get(name, 0), val)
        for name in sorted(best):
            if seen.get((q, name), 0) < best[name]:
                queue[q].wait_ge(T.sem[name], int(best[name]))
                seen[(q, name)] = best[name]

    def needs(q, R, W, own, acc):
        toks = []
        for lst, wr in ((R, False), (W, True)):
            for name, lo, hi in lst:
                psum = name[:2] == "pb"
                for (l2, h2, w2, sem, val, q2) in past.get(name, []):
                    if sem == own and own[:1] == "d":
                        continue
                    same = q2 == q and sem[:1] == "c"
                    if psum and not same:
                        hit = True
                    else:
                        hit = l2 < hi and lo < h2 and (w2 or wr)
                        if same and (not w2 or (wr and acc)):
                            hit = False
                    if hit:
                        toks.append((sem, count[sem] if sem[:1] == "d" else val))
        return toks

    def record(q, R, W, sem, val):
        for lst, wr in ((R, False), (W, True)):
            for name, lo, hi in lst:
                old = past.get(name, [])
                if name[:2] == "pb":
                    old = [a for a in old if a[5] == q]
                elif wr:
                    old = [a for a in old if not (lo <= a[0] and a[1] <= hi and not (a[3] == sem and sem[:1] == "d"))]
                past[name] = old + [(lo, hi, wr, sem, val, q)]

    def op(q, fn, R=(), W=(), acc=False, extra=()):
        sem = "c" + q
        wait(q, needs(q, R, W, sem, acc) + list(extra))
        fn(queue[q]).then_inc(T.sem[sem], 1)
        count[sem] = count.get(sem, 0) + 1
        record(q, R, W, sem, count[sem])

    def dma(q, sem, fn, R=(), W=()):
        wait(q, needs(q, R, W, sem, False))
        fn(queue[q]).then_inc(T.sem[sem], 16)
        count[sem] = count.get(sem, 0) + 16
        record(q, R, W, sem, count[sem])

    def a(name, lo=0, hi=None):
        return (name, lo, SCRATCH[name][1][1] if hi is None else hi)

    def ap(x):
        return T[x[0]][:, x[1]:x[2]]

    def fill(x, val):
        op("v", lambda e: e.memset(ap(x), val), W=[x])

    def ts(out, in0, s1, op0, s2=None, op1=None, R=()):
        if op1 is None:
            op("v", lambda e: e.tensor_scalar(ap(out), ap(in0), s1, None, op0), R=[in0] + list(R), W=[out])
        else:
            op("v", lambda e: e.tensor_scalar(ap(out), ap(in0), s1, s2, op0, op1), R=[in0] + list(R), W=[out])

    def tt(out, in0, in1, o):
        op("v", lambda e: e.tensor_tensor(ap(out), ap(in0), ap(in1), o), R=[in0, in1], W=[out])

    def cp(out, in_):
        op("v", lambda e: e.tensor_copy(ap(out), ap(in_)), R=[in_], W=[out])

    def scp(out, in_, func=F.Copy, scale=1.0):
        op("s", lambda e: e.activation(ap(out), ap(in_), func, scale=scale), R=[in_], W=[out])

    def gat(q, out, win, off):
        if q == "v":
            op("v", lambda e: e.tensor_copy(ap(out), ap(win).indirect(ap(off))), R=[win, off], W=[out])
        else:
            op("s", lambda e: e.activation(ap(out), ap(win).indirect(ap(off)), F.Copy), R=[win, off], W=[out])

    def gtt(out, win, off, in1, o):
        op("v", lambda e: e.tensor_tensor(ap(out), ap(win).indirect(ap(off)), ap(in1), o), R=[win, off, in1], W=[out])

    def sca(win, off, in_):
        op("v", lambda e: e.tensor_copy(ap(win).indirect(ap(off)), ap(in_)), R=[off, in_], W=[win])

    def mm(out, lhsT, rhs, start, stop):
        op("t", lambda e: e.matmul(ap(out), ap(lhsT), ap(rhs), start, stop), R=[lhsT, rhs], W=[out], acc=not start)

    def iota(out, pattern, base, cm, imprecise=False):
        if imprecise:
            op("g", lambda e: e.iota(ap(out), pattern, base, cm, allow_small_or_imprecise_dtypes=True), W=[out])
        else:
            op("g", lambda e: e.iota(ap(out), pattern, base, cm), W=[out])

    def broadcast(sem, out, row):
        dma("g", sem, lambda e: e.indirect_dma_start(ap(out), None, T[row][:], IndirectOffsetOnAxis(ap=T.zI[:, 0:1], axis=0),
                                                     bounds_check=0), R=[a("zI")], W=[out])

    dma("y", "dconn", lambda e: e.dma_start(T.connI[:], T.conn[:]), W=[a("connI")])
    dma("y", "dshare", lambda e: e.dma_start(T.shI[:], T.share[:]), W=[a("shI")])
    dma("y", "dke", lambda e: e.dma_start(T.keB[0:8, :], T.ke[:]), W=[a("keB")])
    for c in range(8):
        dma("y", "du", lambda e, c=c: e.dma_start(T.uwin[16 * c:16 * c + 16, 0:M], T.u[:]), W=[a("uwin", 0, M)])

    H, W3, S3 = 632, 3 * (MW // 4), MW - 632
    fill(a("Wv", 0, H), 0.0)
    fill(a("zI"), 0)
    iota(a("dat", 0, 1024), [[-1, 1024]], E, 0, True)
    iota(a("Wv", W3, MW), [[0, MW - W3]], 0, 0, True)
    iota(a("Ws", S3, MW), [[0, MW - S3]], 0, 0, True)
    iota(a("dat", 1024, 2048), [[-1, 1024]], E - 1024, 0, True)
    broadcast("dstr", a("strep"), "st")
    iota(a("idm"), [[-1, 128]], 128, 1)
    iota(a("pI"), [[0, 2]], 0, 1)
    op("g", lambda e: e.iota(T.asI[0:8, :], [[1, 128]], 128, -16), W=[a("asI")])
    iota(a("dmp0"), [[0, 3], [16, 8]], CB, 1, True)
    iota(a("dat", 2048, ES), [[-1, ES - 2048]], E - 2048, 0, True)
    broadcast("dwr", a("wrep", 0, M), "w")
    iota(a("ADD", 0, MW // 2), [[0, MW // 2]], 0, 0, True)

    scp(a("Ws", 0, H), a("Wv", 0, H), F.Silu)
    for lo, hi in ((H, 2 * H), (2 * H, 4 * H), (4 * H, S3)):
        scp(a("Ws", lo, hi), a("Ws", 0, hi - lo), F.Silu)
    fill(a("Wv", H, 4 * H), 0.0)

    def runs(out, src, i_, n_, t_):
        ts(i_, src, 15, A.bitwise_and)
        ts(n_, src, 1.0 / (16 * RUN - 1), A.mult)
        tt(t_, n_, i_, A.add)
        ts(out, t_, (16 * RUN - 1) / 16.0, A.mult, 0.25, A.add)

    runs(a("piU"), a("connI"), a("piI"), a("piN"), a("piT"))
    fill(a("Wv", 4 * H, W3), 0.0)

    def scat_s(e0, e1):
        off, x = a("piU", e0 // 16, e1 // 16), a("dat", e0, e1)
        op("s", lambda e: e.activation(ap(a("Ws")).indirect(ap(off)), ap(x), F.Silu), R=[off, x], W=[a("Ws")])

    def scat_v(e0, e1):
        off, x = a("piU", e0 // 16, e1 // 16), a("dat", e0 - ES, e1 - ES)
        op("v", lambda e: e.tensor_scalar(ap(a("Wv")).indirect(ap(off)), ap(x), 1.0, float(-ES), A.mult, A.add),
           R=[off, x], W=[a("Wv")])

    scat_s(0, 1024)
    scat_v(ES, ES + 1024)
    scat_s(1024, 2048)
    scat_v(ES + 1024, E)
    scat_s(2048, ES)
    for nm, wn, sem in (("invV", "Wv", "dxv"), ("invS", "Ws", "dxs")):
        for i in range(16):
            dma("y", sem, lambda e, i=i, nm=nm, wn=wn: e.dma_start(T[nm][i:128:16, :], T[wn][i:128:16, RUN * i:RUN * i + NK]),
                R=[a(wn)], W=[a(nm)])

    cp(a("connU"), a("connI"))
    op("v", lambda e: e.tensor_scalar(T.asJ[0:8, :], T.asI[0:8, :], 4, None, A.arith_shift_right), R=[a("asI")], W=[a("asJ")])
    ts(a("idt"), a("idm"), 15, A.bitwise_and)
    op("v", lambda e: e.tensor_scalar(T.asB[0:8, :], T.asJ[0:8, :], 8, None, A.is_equal), R=[a("asJ")], W=[a("asB")])
    op("t", lambda e: e.matmul(T.pb1[0:8, 0:128], T.keB[0:8, 0:8], T.asB[0:8, :], True, True),
       R=[a("keB"), a("asB")], W=[a("pb1", 0, 128)])
    ts(a("PosR"), a("idt"), 0, A.is_equal)
    ts(a("g16"), a("pI"), 4, A.arith_shift_right)
    op("v", lambda e: e.tensor_copy(T.Yb[0:8, :], T.pb1[0:8, 0:128]), R=[a("pb1", 0, 128)], W=[a("Yb")])
    op("t", lambda e: e.matmul(T.pb2[:, 0:128], T.asB[0:8, :], T.Yb[0:8, :], True, True),
       R=[a("asB"), a("Yb")], W=[a("pb2", 0, 128)])
    for k, q in enumerate(partners):
        ts(a("mk", k, k + 1), a("g16", 0, 1), q, A.is_equal)
    tt(a("KlB"), a("pb2", 0, 128), a("PosR"), A.mult)
    for k in range(3):
        ts(a("shM", 8 * k, 8 * k + 8), a("shI"), T.mk[:, k:k + 1], A.mult, R=[a("mk", k, k + 1)])
    mm(a("pb0", 0, 24), a("PosR"), a("shM"), True, True)
    fill(a("uwin", M, MW), 0.0)
    fill(a("wrep", M, MW), 0.0)
    ts(a("IdF"), a("idm"), 128, A.is_equal)
    cp(a("SRi"), a("pb0", 0, 24))
    cp(a("SRu"), a("pb0", 0, 24))
    runs(a("piS"), a("SRi"), a("sqI"), a("sqN"), a("sqT"))

    gat("v", a("O1"), a("Wv"), a("piS"))
    gtt(a("O2"), a("Ws"), a("piS"), a("O1"), A.add)
    for k in range(3):
        tt(a("Om", 128 * k, 128 * k + 128), a("O2", 128 * k, 128 * k + 128), a("PosR"), A.mult)

    def comp_lists(i0, i1):
        for i in range(i0, i1):
            op("t", lambda e, i=i: e.matmul(T.pb3[:, 0:24], T.IdF[:], T.Om[:, i:384:16], i == 0, i == 15),
               R=[a("IdF"), a("Om")], W=[a("pb3", 0, 24)], acc=i > 0)

    def kmul(bank, K, X, x0, x1):
        mm(a(bank, 0, x1 - x0), a(K), a(X, x0, x1), True, True)

    def stmul(bank, x0, x1):
        tt(a("V", x0, x1), a(bank, 0, x1 - x0), a("strep", x0, x1), A.mult)

    for j in range(8):
        x0, x1 = 512 * j, 512 * j + 512
        bank = "pb%d" % (4 + j % 4)
        gat("s", a("X1", x0, x1), a("uwin"), a("connU", 32 * j, 32 * j + 32))
        kmul(bank, "KlB", "X1", x0, x1)
        stmul(bank, x0, x1)
        if j == 0:
            tt(a("KlF"), a("pb2", 0, 128), a("PosR"), A.mult)
            ts(a("IdB"), a("idm"), 128, A.is_equal)
        if 1 <= j <= 4:
            comp_lists(4 * j - 4, 4 * j)
        if j == 1:
            ts(a("NegR"), a("idt"), 0, A.is_equal, -1.0, A.mult)
            fill(a("V", E, E + 8), 0.0)
        if j == 2:
            cp(a("shU"), a("shI"))
            for k in (1, 2):
                fill(a("recv%d" % k, 16 * r, 16 * r + 16), 0.0)
        if j == 4:
            tt(a("invT"), a("invV"), a("invS"), A.add)
        if j == 5:
            ts(a("invU", 0, NK), a("invT"), -1.0, A.mult, E + 0.25, A.add)
            fill(a("invU", NK, 320), E)
        if j == 6:
            ts(a("clU"), a("pb3", 0, 24), -1.0, A.mult, E + 0.25, A.add)
            for c in range(4):
                mm(a("pb%d" % c), a("IdB"), a("uwin", 512 * c, 512 * c + 512), True, False)
    gat("s", a("wslot"), a("wrep"), a("SRu"))
    gat("s", a("uslot"), a("uwin"), a("SRu"))

    VW = a("V")
    FX = a("pb3", 0, 384)
    used, masks = [], {}
    for q in sorted(partners, key=lambda q: len(topo.engines(core, T.cores[q]))):
        ok = [e for e in topo.engines(core, T.cores[q]) if e not in used][:PER]
        used += ok
        masks[q] = sum(1 << e for e in ok)

    def slots():
        gtt(a("S1"), VW, a("clU"), a("wslot"), A.mult)

    def message():
        for k in range(3):
            mm(a("pb7", 16 * k, 16 * k + 16), a("S1", 128 * k, 128 * k + 128), a("PosR", 0, 16), True, True)

    def send(rnd):
        nm = "send%d" % rnd
        wait("g", needs("g", [a(nm)], [], "loc%d" % rnd, False))
        tr = []
        for k, q in enumerate(partners):
            rid, pid, _se = topo.addr(T.cores[q])
            tr.append(RemoteDMATransfer(dst_ids=[DstId(rid=rid, pnc=pid)], dma_engine_mask=masks[q],
                                        remote_sem=T.sem["arr%d" % rnd], src=T[nm][:, 16 * k:16 * k + 16],
                                        dst=T["recv%d" % rnd][:, 16 * r:16 * r + 16]))
        g.remote_dma_fused(tr, local_sem=T.sem["loc%d" % rnd])
        count["loc%d" % rnd] = 3 * PER
        count["arr%d" % rnd] = 3 * PER

    def arrive(rnd):
        nm = "recv%d" % rnd
        op("t", lambda e: e.matmul(T.pb7[0:64, 128:256], T[nm][:, 0:64], T.IdF[:], True, True),
           R=[a(nm), a("IdF")], W=[a("pb7", 128, 256)], extra=[("arr%d" % rnd, 3 * PER)])
        op("s", lambda e: e.activation(T.Rw[0:64, :], T.pb7[0:64, 128:256], F.Copy), R=[a("pb7", 128, 256)], W=[a("Rw")])

    bounds = [(512 * c, min(512 * c + 512, M)) for c in range(10)]
    bank1 = ["pb0", "pb1", "pb2", "pb3", "pb4", "pb5", "pb6", "pb0", "pb1", "pb2"]
    for c, (n0, n1) in enumerate(bounds):
        G, P = a("G", n0, n1), a(bank1[c], 0, n1 - n0)
        gtt(G, VW, a("invU", n0 // 16, n1 // 16), a("wrep", n0, n1), A.mult)
        if c == 1:
            slots()
        if c in (4, 5):
            mm(P, a("IdB"), a("uwin", n0, n1), True, False)
        if c == 2:
            for nm in ("x2c", "wc"):
                op("v", lambda e, nm=nm: e.memset(T[nm][96:128, 448:CB], 0.0), W=[a(nm)])
            op("v", lambda e: e.memset(T.Rw[64:128, :], 0.0), W=[a("Rw")])
        if c == 9:
            sca(a("ADD"), a("shU"), a("Rw"))
            gat("s", a("D1"), a("ADD"), a("SRu"))
            mm(FX, a("NegR"), a("D1"), False, True)
        mm(P, a("NegR"), G, c > 5, True)
        if c == 1:
            message()
            scp(a("send1"), a("pb7", 0, 48))
            send(1)
        if c < 6:
            scp(a("win", n0, n1), P)
        if c < 4:
            z0 = MW // 2 + c * H
            scp(a("ADD", z0, z0 + H), a("uwin", 0, H), F.Copy, 0.0)
        if c == 6:
            arrive(1)
        if c == 7:
            mm(FX, a("NegR"), a("S1"), True, False)
        if c > 7:
            for k in ((6, 7) if c == 8 else (8, 9)):
                if c == 8:
                    continue
                n0, n1 = bounds[k - 2]
                tt(a("win", n0, n1), a("uwin", n0, n1), a(bank1[k - 2], 0, n1 - n0), A.add)
    tt(a("win", *bounds[8]), a("uwin", *bounds[8]), a(bank1[8]), A.add)
    tt(a("x2s"), a("uslot"), FX, A.add)
    tt(a("win", *bounds[9]), a("uwin", *bounds[9]), a(bank1[9], 0, bounds[9][1] - bounds[9][0]), A.add)
    for k in range(3):
        sca(a("win"), a("SRu", 8 * k, 8 * k + 8), a("x2s", 128 * k, 128 * k + 128))
    for nm, src, sem in (("wc", "wrep", "dwc"), ("x2c", "win", "dx2")):
        for c in range(8):
            n = min(CB, M - CB * c)
            dma("y", sem, lambda e, c=c, n=n, nm=nm, src=src: e.dma_start(
                T[nm][16 * c:16 * c + 16, 0:n], T[src][16 * c:16 * c + 16, CB * c:CB * c + n]), R=[a(src, 0, M)], W=[a(nm)])

    def perm(lo, hi):
        for k in range(lo, hi):
            aa, jj, i4 = k // 4, k // 2 % 2, k % 2
            s, t = 8 * jj + 2 * aa + i4, 40 * (2 * aa + jj) + i4
            op("v", lambda e, s=s, t=t: e.tensor_copy(T.invP[:, s:320:16], T.invU[:, t:t + 39:2]),
               R=[a("invU")], W=[a("invP")], acc=True)

    def compact():
        ts(a("mk", 4, 5), a("g16", 0, 1), float(CB), A.mult)
        ts(a("mk", 5, 6), a("g16", 0, 1), 16.0, A.mult)
        ts(a("c1"), a("SRi"), T.mk[:, 4:5], A.subtract, R=[a("mk", 4, 5)])
        ts(a("dmp"), a("dmp0"), T.mk[:, 5:6], A.subtract, R=[a("mk", 5, 6)])
        ts(a("c2"), a("c1"), 0.0, A.is_ge)
        ts(a("c3"), a("c1"), float(CB), A.is_lt)
        tt(a("c4"), a("c1"), a("dmp"), A.subtract)
        tt(a("c2"), a("c2"), a("c3"), A.mult)
        tt(a("c4"), a("c4"), a("c2"), A.mult)
        tt(a("c4"), a("c4"), a("dmp"), A.add)
        cp(a("cpU"), a("c4"))

    cuts = [0, 256, 512] + [512 * k for k in range(2, 8)] + [3840, 4096]
    for j in range(len(cuts) - 1):
        x0, x1 = cuts[j], cuts[j + 1]
        bank = "pb%d" % (0, 1, 2, 4, 5, 6)[j % 6]
        gat("v" if j == 0 else "s", a("X2", x0, x1), a("win", 0, M), a("connU", x0 // 16, x1 // 16))
        kmul(bank, "KlF", "X2", x0, x1)
        if j == 0:
            perm(0, 8)
        stmul(bank, x0, x1)
        if j in (1, 2):
            perm(4 + 4 * j, 8 + 4 * j)
        if j == 3:
            op("v", lambda e: e.transpose(T.wT[:], T.wc[:]), R=[a("wc")], W=[a("wT")])
        if j == 4:
            op("v", lambda e: e.transpose(T.xT[:], T.x2c[:]), R=[a("x2c")], W=[a("xT")])
        if j == 5:
            compact()

    parts = [(0, 256, "pb0"), (256, 512, "pb1"), (512, 640, "pb2")]

    def finish(k):
        lo, hi, bank = parts[k]
        tt(a("yt", lo, hi), a(bank, 0, hi - lo), a("wT", lo, hi), A.mult)
        tt(a("yu", lo, hi), a("xT", lo, hi), a("yt", lo, hi), A.subtract)
        op("v", lambda e: e.transpose(T.Y[:, lo:hi], T.yu[:, lo:hi]), R=[a("yu", lo, hi)], W=[a("Y", lo, hi)])

    pieces = [("s", 0), ("v", 512), ("s", 768), ("s", 1280), ("v", 1792), ("s", 2304), ("s", 2816), ("v", 3328), ("s", 3840),
              ("s", 4352), ("v", 4864)]
    slots()
    message()
    for k, (q, lo) in enumerate(pieces):
        hi = (pieces + [("", 8 * CB)])[k + 1][1]
        gat(q, a("G", lo, hi), VW, a("invP", lo // 16, hi // 16))
        if k == 1:
            cp(a("send2"), a("pb7", 0, 48))
            send(2)
        for b in range(lo // 128, hi // 128):
            p0, p1, bank = parts[b // 16]
            o = 16 * b - p0
            mm(a(bank, o, o + 16), a("G", 128 * b, 128 * b + 128), a("PosR", 0, 16), True, True)
        if k == 6:
            mm(FX, a("NegR"), a("S1"), True, False)
        if k == 8:
            arrive(2)
    finish(0)
    sca(a("ADD"), a("shU"), a("Rw"))
    gat("s", a("D1"), a("ADD"), a("SRu"))
    mm(FX, a("NegR"), a("D1"), False, True)
    finish(1)
    finish(2)
    tt(a("x3s"), a("x2s"), FX, A.add)
    for k in range(3):
        sca(a("Y"), a("cpU", 8 * k, 8 * k + 8), a("x3s", 128 * k, 128 * k + 128))
    for c in range(8):
        n = min(CB, M - CB * c)
        dma("y" if c % 2 == 0 else "s", "dy",
            lambda e, c=c, n=n: e.dma_start(T.y[:, CB * c:CB * c + n], T.Y[16 * c:16 * c + 16, 0:n]), R=[a("Y", 0, CB)])

    wait("g", [(name, count[name]) for name in sorted(count)])
